import numpy as np
import ml_dtypes


def mxq(x, axis, fmt="e4m3"):
    dtype, down = {"e4m3": (ml_dtypes.float8_e4m3fn, 7), "e5m2": (ml_dtypes.float8_e5m2, 14)}[fmt]
    v = np.moveaxis(np.asarray(x, np.float32).astype(ml_dtypes.bfloat16).astype(np.float64), axis, -1)
    blocks = v.reshape(v.shape[:-1] + (-1, 32))
    amax = np.abs(blocks).max(-1, keepdims=True)
    byte = np.maximum(np.where(amax > 0, np.frexp(amax)[1] - 1 + 127, 0) - down, 1)
    scale = np.exp2(byte - 127.0)
    codes = (blocks / scale).astype(np.float32).astype(dtype).astype(np.float64)
    return np.moveaxis((codes * scale).reshape(v.shape), -1, axis)


WIDE = False


def mx_kscale(k):
    if not WIDE:
        return np.ones(k)
    levels = np.array([10, -10, 5, -5, 0])
    if k % 512:
        return np.exp2(np.random.permutation(np.resize(levels, k // 32))).repeat(32)
    a = np.empty((k // 512, 16))
    for p in range(k // 512):
        a[p, :8] = np.random.permutation(np.resize(levels, 8))
        for g in range(8):
            far = levels[np.abs(levels - a[p, g]) >= 10]
            a[p, g + 8] = far[np.random.randint(len(far))]
    return np.exp2(a.ravel()).repeat(32)


def f64(x):
    return np.asarray(x).astype(np.float64)


def striped(idx):
    return np.tile(idx.reshape(-1, 16).T, (8, 1)).astype(np.uint16)


def unstriped(offs):
    return offs[:16].T.reshape(-1).astype(np.int64)


E2M1 = np.array([0.0, 0.5, 1.0, 1.5, 2.0, 3.0, 4.0, 6.0, -0.0, -0.5, -1.0, -1.5, -2.0, -3.0, -4.0, -6.0])


def pack_weight(w, fmt):
    k, n = w.shape
    w = f64(np.asarray(w, np.float32).astype(ml_dtypes.bfloat16)).reshape(k // 32, 32, n)
    amax = np.abs(w).max(1)
    if fmt == "e4m3":
        byte = np.frexp(amax)[1] - 1 + 127 - 7
    else:
        mant, ex = np.frexp(amax / 6.0)
        byte = np.where(mant > 0.5, ex, ex - 1) + 127
    byte = np.clip(np.where(amax > 0, byte, 1), 1, 254)
    scaled = (w * np.exp2(127.0 - byte)[:, None, :]).reshape(k, n).astype(np.float32)
    by_word = np.ascontiguousarray(scaled.reshape(k // 512, 128, 4, n).transpose(0, 1, 3, 2))
    if fmt == "e4m3":
        words = by_word.astype(ml_dtypes.float8_e4m3fn).view(np.uint8)
    else:
        c = by_word.astype(ml_dtypes.float4_e2m1fn).view(np.uint8) & 0xF
        words = (c[..., 0::2] | (c[..., 1::2] << 4)).reshape(k // 512, 128, 2 * n)
    return np.ascontiguousarray(words), np.ascontiguousarray(byte.astype(np.uint8).reshape(k // 512, 16, n))


def unpack_weight(words, scales, fmt):
    g, _, n = scales.shape
    words = np.ascontiguousarray(words).reshape(g, 128, n, -1)
    if fmt == "e4m3":
        vals = words.view(ml_dtypes.float8_e4m3fn).astype(np.float64)
    else:
        nib = np.empty((g, 128, n, 4), np.uint8)
        nib[..., 0::2] = words & 0xF
        nib[..., 1::2] = words >> 4
        vals = E2M1[nib]
    vals = vals * np.repeat(np.exp2(scales.astype(np.float64) - 127.0), 8, axis=1)[..., None]
    return vals.transpose(0, 1, 3, 2).reshape(g * 512, n)


def gelu(v):
    return 0.5 * v * (1.0 + np.tanh(np.sqrt(2.0 / np.pi) * (v + 0.044715 * v**3)))


K, T, H, S, T3, S2, P = 1024, 2048, 1024, 1024, 2048, 512, 512

def setup_inputs():
    n = np.random.standard_normal
    ks = mx_kscale(K)[:, None]
    u = mx_kscale(H)[:, None]
    d = {}
    d["tab_words"], d["tab_scales"] = pack_weight(n((K, T)) * ks, "e4m3")
    d["offs"] = striped(np.random.permutation(T)[:S])
    d["w1"] = (1.4 * n((K, H)) / K ** 0.5 / ks * u.T).astype(np.float32)
    d["w4_words"], d["w4_scales"] = pack_weight(n((K, H)) / K ** 0.5 / ks, "e2m1")
    d["unit2"] = (np.exp(0.3 * n(H)) * u[:, 0] ** 2).astype(np.float32)
    d["tab2_words"], d["tab2_scales"] = pack_weight(n((H, T3)) / H ** 0.5 / u, "e4m3")
    d["offs2"] = striped(np.random.permutation(T3)[:S2])
    d["pos1"] = striped(np.random.permutation(S)[:P])
    d["pos2"] = striped(np.random.permutation(S)[:P])
    d["req"] = (1.5 * n((S2, P))).astype(np.float32)
    return d

def reference(tab_words, tab_scales, offs, w1, w4_words, w4_scales, unit2,
              tab2_words, tab2_scales, offs2, pos1, pos2, req):
    v = unpack_weight(tab_words, tab_scales, "e4m3")[:, unstriped(offs)]
    v2 = unpack_weight(tab2_words, tab2_scales, "e4m3")[:, unstriped(offs2)]
    w4 = unpack_weight(w4_words, w4_scales, "e2m1")
    st = mxq(f64(w1), 0, "e4m3").T @ v
    b = w4.T @ v
    size = np.sqrt(np.square(st) + f64(unit2)[:, None])
    h = size * b + st
    e = v2.T @ mxq(h, 0, "e4m3")
    early = e[:, unstriped(pos1)]
    late = e[:, unstriped(pos2)]
    return np.maximum(early, late) + f64(req)

@@ -1,0 +1,294 @@
+from contextlib import ExitStack
+
+import concourse.mybir as mybir
+
+K, T, H, S, T3, S2, PAIRS = 1024, 2048, 1024, 1024, 2048, 512, 512
+FLOPS = 2 * (2 * K * H * S + H * S2 * S)
+
+F32 = mybir.dt.float32
+BF16 = mybir.dt.bfloat16
+I32 = mybir.dt.int32
+U32 = mybir.dt.uint32
+U16 = mybir.dt.uint16
+U8 = mybir.dt.uint8
+FP8X4 = mybir.dt.float8_e4m3fn_x4
+FP4X4 = mybir.dt.float4_e2m1fn_x4
+ACT = mybir.ActivationFunctionType
+ALU = mybir.AluOpType
+
+P = 128
+PACK = 4
+KP = P * PACK
+PASSES = 2
+STEP = 256
+STEPS = S // STEP
+HALF = STEP // 2
+LIST_COL = 16
+
+
+def tile_list_concrete_recipe_scores_kernel(
+    tc, tab_words, tab_scales, offs, w1, w4_words, w4_scales, unit2,
+    tab2_words, tab2_scales, offs2, pos1, pos2, req, out,
+):
+    nc = tc.nc
+    with ExitStack() as ctx:
+        keep = ctx.enter_context(tc.tile_pool(name="keep", bufs=1))
+        ring = ctx.enter_context(tc.tile_pool(name="ring", bufs=3))
+        psum = ctx.enter_context(tc.psum_pool(name="psum", bufs=1))
+
+        def held(name, shape, dtype):
+            return keep.tile(shape, dtype, name=name, align_bytes=64)
+
+        def reused(name, tag, shape, dtype):
+            return keep.tile(shape, dtype, name=name, tag=tag, align_bytes=64)
+
+        def per(name, count, shape, dtype):
+            return [held("%s%d" % (name, n), shape, dtype) for n in range(count)]
+
+        offs_t = held("offs_t", [P, S // LIST_COL], U16)
+        offs2_t = held("offs2_t", [P, S2 // LIST_COL], U16)
+        pos1_t = held("pos1_t", [P, PAIRS // LIST_COL], U16)
+        pos2_t = held("pos2_t", [P, PAIRS // LIST_COL], U16)
+
+        tab_w = per("tab_w", PASSES, [P, T], U32)
+        tab_s = held("tab_s", [P, PASSES * T], U8)
+        tab2_w = per("tab2_w", PASSES, [P, T3], U32)
+        tab2_s = held("tab2_s", [P, T3], U8)
+        v_w0 = held("v_w0", [P, S], U32)
+        v_w1_first = held("v_w1_first", [P, STEP], U32)
+        v_s = per("v_s", PASSES, [P, S], U8)
+        w4_raw = per("w4_raw", PASSES, [P, PASSES, 2 * KP], U8)
+        w4_raw_s = held("w4_raw_s", [P, PASSES, H], U8)
+        w4_w = per("w4_w", PASSES, [P, PASSES, PACK, 2 * P], U8)
+        w4_s = per("w4_s", PASSES, [P, PASSES, PACK, P], U8)
+        w1_raw = [per("w1_raw%d_" % b, PASSES, [P, PACK, KP], F32) for b in range(PASSES)]
+        w1_bf = {(b, a): held("w1_bf%d%d" % (b, a), [P, PACK * KP], BF16) for b, a in ((0, 0), (0, 1), (1, 0))}
+        w1_w = {(b, a): held("w1_w%d%d" % (b, a), [P, KP], U32) for b, a in ((0, 0), (0, 1), (1, 1))}
+        late = {}
+        w1_s = [per("w1_s%d_" % b, PASSES, [P, KP], U8) for b in range(PASSES)]
+        unit_t = held("unit_t", [P, PASSES, PACK], F32)
+        h_w = per("h_w", PASSES, [P, S], U32)
+        h_s = per("h_s", PASSES, [P, S], U8)
+        scores = per("scores", S2 // P, [P, S], F32)
+        req_t = held("req_t", [P, S2 // P, PAIRS], F32)
+
+        def load_words(dst, src):
+            nc.sync.dma_start(out=dst[:].bitcast(I32), in_=src.rearrange("p t i -> p (t i)").bitcast(I32))
+
+        def load_w1(b, a):
+            rows = w1[a * KP:(a + 1) * KP, b * KP:(b + 1) * KP]
+            nc.sync.dma_start(out=w1_raw[b][a][:], in_=rows.rearrange("(p j) c -> p j c", j=PACK))
+
+        def load_w4(b):
+            src = w4_words[:, :, 2 * KP * b:2 * KP * (b + 1)].rearrange("a p c -> p a c")
+            nc.sync.dma_start(out=w4_raw[b][:].bitcast(I32), in_=src.bitcast(I32))
+
+        nc.gpsimd.memset(tab_s[:].bitcast(I32), 0)
+        nc.gpsimd.memset(w4_raw_s[:].rearrange("p a c -> p (a c)").bitcast(I32), 0)
+        nc.gpsimd.memset(tab2_s[:].bitcast(I32), 0)
+
+        nc.sync.dma_start(offs_t[:], offs)
+        for q in range(4):
+            nc.sync.dma_start(
+                out=tab_s[32 * q:32 * q + 4, :].rearrange("r (a t) -> r a t", a=PASSES).bitcast(I32),
+                in_=tab_scales[:, 4 * q:4 * q + 4, :].rearrange("a r t -> r a t").bitcast(I32))
+        load_w1(0, 0)
+        load_words(tab_w[0], tab_words[0])
+        load_w1(0, 1)
+        load_words(tab_w[1], tab_words[1])
+        load_w4(0)
+        for q in range(4):
+            nc.sync.dma_start(
+                out=w4_raw_s[32 * q:32 * q + 4, :, :].bitcast(I32),
+                in_=w4_scales[:, 4 * q:4 * q + 4, :].rearrange("a r c -> r a c").bitcast(I32))
+        nc.sync.dma_start(out=unit_t[:], in_=unit2.rearrange("(b p i) -> p b i", b=PASSES, i=PACK))
+        load_w4(1)
+        load_w1(1, 0)
+        load_w1(1, 1)
+        for q in range(4):
+            nc.sync.dma_start(
+                out=tab2_s[32 * q:32 * q + 8, :].bitcast(I32),
+                in_=tab2_scales[:, 4 * q:4 * q + 4, :].bitcast(I32))
+        nc.sync.dma_start(offs2_t[:], offs2)
+        load_words(tab2_w[0], tab2_words[0])
+        load_words(tab2_w[1], tab2_words[1])
+        nc.sync.dma_start(pos1_t[:], pos1)
+        nc.sync.dma_start(pos2_t[:], pos2)
+        nc.sync.dma_start(out=req_t[:], in_=req.rearrange("(m p) j -> p m j", p=P))
+
+        def v_words(a, lo, hi):
+            if a == 0:
+                return v_w0[:, lo:hi]
+            if hi <= STEP:
+                return v_w1_first[:, lo:hi]
+            return late["v_w1"][:, lo - STEP:hi - STEP]
+
+        def gather(dst, window, offsets, lo, hi):
+            nc.vector.tensor_copy(
+                dst, window.indirect(offsets[:, lo // LIST_COL:hi // LIST_COL]))
+
+        def deal_w4(b):
+            nc.scalar.copy(
+                out=w4_w[b][:].bitcast(U16),
+                in_=w4_raw[b][:].bitcast(U16).rearrange("p a (m i) -> p a i m", i=PACK))
+            nc.gpsimd.tensor_copy(
+                out=w4_s[b][:],
+                in_=w4_raw_s[:, :, b * KP:(b + 1) * KP].rearrange("p a (m i) -> p a i m", i=PACK))
+
+        def round_w1(engine, b, a, lo, hi):
+            dst = w1_bf[b, a][:].rearrange("p (i m j) -> p m j i", i=PACK, j=PACK)[:, lo:hi]
+            src = w1_raw[b][a][:].rearrange("p j (m i) -> p m j i", i=PACK)[:, lo:hi]
+            if engine == "scalar":
+                nc.scalar.copy(out=dst, in_=src)
+            elif engine == "vector":
+                nc.vector.tensor_copy(out=dst, in_=src)
+            else:
+                nc.gpsimd.tensor_copy(
+                    out=dst.rearrange("p m j i -> p i m j"), in_=src.rearrange("p m j i -> p i m j"))
+
+        def quantize_w1(b, a):
+            nc.vector.quantize_mx(out=w1_w[b, a][:].bitcast(FP8X4), scales=w1_s[b][a][:], in_=w1_bf[b, a][:])
+
+        def bank(tag, depth):
+            return psum.tile([P, 512], F32, name=tag, tag=tag, bufs=depth)
+
+        state = {}
+
+        def products(n):
+            b, c = divmod(n, STEPS)
+            st_banks, b_banks = [], []
+            for u in range(2):
+                acc = bank("st", 5)
+                cols = slice(c * STEP + u * HALF, c * STEP + (u + 1) * HALF)
+                for a in range(PASSES):
+                    for i in range(PACK):
+                        nc.tensor.matmul_mx(
+                            out=acc[:, i * HALF:(i + 1) * HALF],
+                            lhsT=w1_w[b, a][:, i * P:(i + 1) * P].bitcast(FP8X4),
+                            lhsT_scale=w1_s[b][a][:, i * P:(i + 1) * P],
+                            rhs=v_words(a, cols.start, cols.stop).bitcast(FP8X4), rhs_scale=v_s[a][:, cols],
+                            start=(a == 0 and i == 0), stop=(a == PASSES - 1 and i == PACK - 1))
+                st_banks.append(acc)
+            cols = slice(c * STEP, (c + 1) * STEP)
+            for w in range(2):
+                acc = bank("bb", 3)
+                for a in range(PASSES):
+                    for x in range(2):
+                        i = 2 * w + x
+                        nc.tensor.matmul_mx(
+                            out=acc[:, x * STEP:(x + 1) * STEP],
+                            lhsT=w4_w[b][:, a, i, :].bitcast(FP4X4), lhsT_scale=w4_s[b][:, a, i, :],
+                            rhs=v_words(a, cols.start, cols.stop).bitcast(FP8X4), rhs_scale=v_s[a][:, cols],
+                            start=(a == 0 and x == 0), stop=(a == PASSES - 1 and x == 1))
+                b_banks.append(acc)
+            square = reused("square", "square%d" % n, [P, PACK, STEP], F32)
+            size = reused("size", "size%d" % (n % 4), [P, PACK, STEP], F32)
+            for u in range(2):
+                nc.scalar.activation(
+                    out=square[:, :, u * HALF:(u + 1) * HALF],
+                    in_=st_banks[u][:].rearrange("p (i j) -> p i j", i=PACK), func=ACT.Square)
+            for i in range(PACK):
+                nc.scalar.activation(
+                    out=size[:, i, :], in_=square[:, i, :], func=ACT.Sqrt, bias=unit_t[:, b, i:i + 1])
+            scaled = ring.tile([P, PACK, STEP], F32, name="scaled")
+            h_bf = ring.tile([P, STEP * PACK], BF16, name="h_bf", align_bytes=64)
+            state[n] = (st_banks, b_banks, size, scaled, h_bf)
+
+        def scale_step(n, w):
+            st_banks, b_banks, size, scaled, h_bf = state[n]
+            nc.vector.tensor_tensor(
+                scaled[:, 2 * w:2 * w + 2, :].rearrange("p x j -> p (x j)"), b_banks[w][:],
+                size[:, 2 * w:2 * w + 2, :].rearrange("p x j -> p (x j)"), ALU.mult)
+
+        def skip_step(n, u):
+            st_banks, b_banks, size, scaled, h_bf = state[n]
+            dst = h_bf[:, u * HALF * PACK:(u + 1) * HALF * PACK]
+            nc.vector.tensor_tensor(
+                dst.rearrange("p (g j i) -> p g i j", j=4, i=PACK),
+                st_banks[u][:].rearrange("p (i g j) -> p g i j", i=PACK, j=4),
+                scaled[:, :, u * HALF:(u + 1) * HALF].rearrange("p i (g j) -> p g i j", j=4),
+                ALU.add)
+
+        def quantize_h(n, lo, hi):
+            b, c = divmod(n, STEPS)
+            h_bf = state[n][4]
+            cols = slice(c * STEP + lo, c * STEP + hi)
+            nc.vector.quantize_mx(
+                out=h_w[b][:, cols].bitcast(FP8X4), scales=h_s[b][:, cols],
+                in_=h_bf[:, lo * PACK:hi * PACK])
+
+        def score(m, lo, hi, tag, depth):
+            acc = bank(tag, depth)
+            rows = slice(m * P, (m + 1) * P)
+            for b in range(PASSES):
+                nc.tensor.matmul_mx(
+                    out=acc[:, 0:hi - lo],
+                    lhsT=late["v2_w", b][:, rows].bitcast(FP8X4), lhsT_scale=late["v2_s"][4 * b:P, rows],
+                    rhs=h_w[b][:, lo:hi].bitcast(FP8X4), rhs_scale=h_s[b][:, lo:hi],
+                    start=(b == 0), stop=(b == PASSES - 1))
+            nc.scalar.copy(out=scores[m][:, lo:hi], in_=acc[:, 0:hi - lo])
+
+        round_w1("scalar", 0, 0, 0, P)
+        for a in range(PASSES):
+            gather(v_s[a][:], tab_s[:, a * T:(a + 1) * T], offs_t, 0, S)
+        gather(v_w0[:], tab_w[0][:], offs_t, 0, S)
+        quantize_w1(0, 0)
+        round_w1("scalar", 0, 1, 0, P)
+        gather(v_w1_first[:], tab_w[1][:], offs_t, 0, STEP)
+        quantize_w1(0, 1)
+        late["v_w1"] = reused("v_w1", "w1_bf01", [P, S - STEP], U32)
+        for c in range(1, STEPS):
+            gather(v_words(1, c * STEP, (c + 1) * STEP), tab_w[1][:], offs_t, c * STEP, (c + 1) * STEP)
+        deal_w4(0)
+        for lo in range(0, P, 32):
+            round_w1("gpsimd", 1, 0, lo, lo + 32)
+
+        last = PASSES * STEPS - 1
+        for n in range(last + 1):
+            products(n)
+            scale_step(n, 0)
+            if n > 0:
+                skip_step(n - 1, 1)
+            scale_step(n, 1)
+            if n > 0:
+                quantize_h(n - 1, 0, STEP)
+            skip_step(n, 0)
+            if n == 0:
+                w1_bf[1, 1] = reused("w1_bf11", "square0", [P, PACK * KP], BF16)
+                round_w1("scalar", 1, 1, 0, 32)
+                deal_w4(1)
+            if n == 1:
+                round_w1("scalar", 1, 1, 32, 64)
+                round_w1("vector", 1, 1, 64, P)
+                w1_w[1, 0] = reused("w1_w10", "square1", [P, KP], U32)
+                quantize_w1(1, 0)
+                quantize_w1(1, 1)
+            if n == 4:
+                late["v2_s"] = reused("v2_s", "square3", [P, S2], U8)
+                gather(late["v2_s"][:], tab2_s[:], offs2_t, 0, S2)
+            if n in (5, 6):
+                late["v2_w", n - 5] = reused("v2_w", "square%d" % (n - 1), [P, S2], U32)
+                gather(late["v2_w", n - 5][:], tab2_w[n - 5][:], offs2_t, 0, S2)
+        skip_step(last, 1)
+        quantize_h(last, 0, HALF)
+        quantize_h(last, HALF, STEP)
+
+        for lo, hi in ((0, 512), (512, 768), (768, 896), (896, 1024)):
+            score(0, lo, hi, "bb", 3)
+        for m in range(1, S2 // P):
+            for lo in (0, 512):
+                score(m, lo, lo + 512, "st", 5)
+
+        for m in range(S2 // P):
+            pieces = 2 if m == S2 // P - 1 else 1
+            width = PAIRS // pieces
+            for lo in range(0, PAIRS, width):
+                cols = slice(lo, lo + width)
+                part = slice(lo // LIST_COL, (lo + width) // LIST_COL)
+                early = ring.tile([P, width], F32, name="early")
+                later = ring.tile([P, width], F32, name="later")
+                best = ring.tile([P, width], F32, name="best")
+                nc.vector.tensor_tensor(early[:], scores[m][:].indirect(pos1_t[:, part]), req_t[:, m, cols], ALU.add)
+                nc.vector.tensor_tensor(later[:], scores[m][:].indirect(pos2_t[:, part]), req_t[:, m, cols], ALU.add)
+                nc.vector.tensor_tensor(best[:], early[:], later[:], ALU.max)
+                nc.sync.dma_start(out=out[m * P:(m + 1) * P, cols], in_=best[:])

@@ -34,6 +34,7 @@ def tile_list_concrete_recipe_scores_kernel(
     with ExitStack() as ctx:
         keep = ctx.enter_context(tc.tile_pool(name="keep", bufs=1))
         ring = ctx.enter_context(tc.tile_pool(name="ring", bufs=3))
+        shared = ctx.enter_context(tc.tile_pool(name="shared", bufs=1))
         psum = ctx.enter_context(tc.psum_pool(name="psum", bufs=1))
 
         def held(name, shape, dtype):
@@ -51,17 +52,19 @@ def tile_list_concrete_recipe_scores_kernel(
         pos2_t = held("pos2_t", [P, PAIRS // LIST_COL], U16)
 
         tab_w = per("tab_w", PASSES, [P, T], U32)
-        tab_s = held("tab_s", [P, PASSES * T], U8)
+        tab_s = held("tab_s", [P, T], U8)
         tab2_w = per("tab2_w", PASSES, [P, T3], U32)
         tab2_s = held("tab2_s", [P, T3], U8)
         v_w0 = held("v_w0", [P, S], U32)
         v_w1_first = held("v_w1_first", [P, STEP], U32)
-        v_s = per("v_s", PASSES, [P, S], U8)
+        v_s = held("v_s", [P, S], U8)
+        v_s_low = held("v_s_low", [P, S], U8)
         w4_raw = per("w4_raw", PASSES, [P, PASSES, 2 * KP], U8)
         w4_raw_s = held("w4_raw_s", [P, PASSES, H], U8)
-        w4_w = per("w4_w", PASSES, [P, PASSES, PACK, 2 * P], U8)
+        w4_w = {}
         w4_s = per("w4_s", PASSES, [P, PASSES, PACK, P], U8)
-        w1_raw = [per("w1_raw%d_" % b, PASSES, [P, PACK, KP], F32) for b in range(PASSES)]
+        w1_raw = {(b, a): held("w1_raw%d%d" % (b, a), [P, PACK, KP], F32) for b, a in ((0, 0), (1, 0), (1, 1))}
+        w1_raw[0, 1] = shared.tile([P, PACK, KP], F32, name="w1_raw01", align_bytes=64, offset=0)
         w1_bf = {(b, a): held("w1_bf%d%d" % (b, a), [P, PACK * KP], BF16) for b, a in ((0, 0), (0, 1), (1, 0))}
         w1_w = {(b, a): held("w1_w%d%d" % (b, a), [P, KP], U32) for b, a in ((0, 0), (0, 1), (1, 1))}
         late = {}
@@ -77,7 +80,7 @@ def tile_list_concrete_recipe_scores_kernel(
 
         def load_w1(b, a):
             rows = w1[a * KP:(a + 1) * KP, b * KP:(b + 1) * KP]
-            nc.sync.dma_start(out=w1_raw[b][a][:], in_=rows.rearrange("(p j) c -> p j c", j=PACK))
+            nc.sync.dma_start(out=w1_raw[b, a][:], in_=rows.rearrange("(p j) c -> p j c", j=PACK))
 
         def load_w4(b):
             src = w4_words[:, :, 2 * KP * b:2 * KP * (b + 1)].rearrange("a p c -> p a c")
@@ -85,15 +88,17 @@ def tile_list_concrete_recipe_scores_kernel(
 
         nc.gpsimd.memset(tab_s[:].bitcast(I32), 0)
         nc.gpsimd.memset(w4_raw_s[:].rearrange("p a c -> p (a c)").bitcast(I32), 0)
+        nc.gpsimd.memset(v_s_low[:].bitcast(I32), 0)
         nc.gpsimd.memset(tab2_s[:].bitcast(I32), 0)
 
         nc.sync.dma_start(offs_t[:], offs)
+        load_words(tab_w[0], tab_words[0])
+        nc.sync.dma_start(offs2_t[:], offs2)
         for q in range(4):
             nc.sync.dma_start(
-                out=tab_s[32 * q:32 * q + 4, :].rearrange("r (a t) -> r a t", a=PASSES).bitcast(I32),
-                in_=tab_scales[:, 4 * q:4 * q + 4, :].rearrange("a r t -> r a t").bitcast(I32))
+                out=tab_s[32 * q:32 * q + 8, :].bitcast(I32),
+                in_=tab_scales[:, 4 * q:4 * q + 4, :].bitcast(I32))
         load_w1(0, 0)
-        load_words(tab_w[0], tab_words[0])
         load_w1(0, 1)
         load_words(tab_w[1], tab_words[1])
         load_w4(0)
@@ -102,19 +107,6 @@ def tile_list_concrete_recipe_scores_kernel(
                 out=w4_raw_s[32 * q:32 * q + 4, :, :].bitcast(I32),
                 in_=w4_scales[:, 4 * q:4 * q + 4, :].rearrange("a r c -> r a c").bitcast(I32))
         nc.sync.dma_start(out=unit_t[:], in_=unit2.rearrange("(b p i) -> p b i", b=PASSES, i=PACK))
-        load_w4(1)
-        load_w1(1, 0)
-        load_w1(1, 1)
-        for q in range(4):
-            nc.sync.dma_start(
-                out=tab2_s[32 * q:32 * q + 8, :].bitcast(I32),
-                in_=tab2_scales[:, 4 * q:4 * q + 4, :].bitcast(I32))
-        nc.sync.dma_start(offs2_t[:], offs2)
-        load_words(tab2_w[0], tab2_words[0])
-        load_words(tab2_w[1], tab2_words[1])
-        nc.sync.dma_start(pos1_t[:], pos1)
-        nc.sync.dma_start(pos2_t[:], pos2)
-        nc.sync.dma_start(out=req_t[:], in_=req.rearrange("(m p) j -> p m j", p=P))
 
         def v_words(a, lo, hi):
             if a == 0:
@@ -137,7 +129,7 @@ def tile_list_concrete_recipe_scores_kernel(
 
         def round_w1(engine, b, a, lo, hi):
             dst = w1_bf[b, a][:].rearrange("p (i m j) -> p m j i", i=PACK, j=PACK)[:, lo:hi]
-            src = w1_raw[b][a][:].rearrange("p j (m i) -> p m j i", i=PACK)[:, lo:hi]
+            src = w1_raw[b, a][:].rearrange("p j (m i) -> p m j i", i=PACK)[:, lo:hi]
             if engine == "scalar":
                 nc.scalar.copy(out=dst, in_=src)
             elif engine == "vector":
@@ -160,14 +152,18 @@ def tile_list_concrete_recipe_scores_kernel(
             for u in range(2):
                 acc = bank("st", 5)
                 cols = slice(c * STEP + u * HALF, c * STEP + (u + 1) * HALF)
-                for a in range(PASSES):
-                    for i in range(PACK):
-                        nc.tensor.matmul_mx(
-                            out=acc[:, i * HALF:(i + 1) * HALF],
-                            lhsT=w1_w[b, a][:, i * P:(i + 1) * P].bitcast(FP8X4),
-                            lhsT_scale=w1_s[b][a][:, i * P:(i + 1) * P],
-                            rhs=v_words(a, cols.start, cols.stop).bitcast(FP8X4), rhs_scale=v_s[a][:, cols],
-                            start=(a == 0 and i == 0), stop=(a == PASSES - 1 and i == PACK - 1))
+                if n == 0:
+                    order = [(a, i) for a in range(PASSES) for i in range(PACK)]
+                else:
+                    order = [(a, i) for i in range(PACK) for a in range(PASSES)]
+                for a, i in order:
+                    nc.tensor.matmul_mx(
+                        out=acc[:, i * HALF:(i + 1) * HALF],
+                        lhsT=w1_w[b, a][:, i * P:(i + 1) * P].bitcast(FP8X4),
+                        lhsT_scale=w1_s[b][a][:, i * P:(i + 1) * P],
+                        rhs=v_words(a, cols.start, cols.stop).bitcast(FP8X4),
+                        rhs_scale=v_s[4 * a:P, cols],
+                        start=((a, i) == order[0]), stop=((a, i) == order[-1]))
                 st_banks.append(acc)
             cols = slice(c * STEP, (c + 1) * STEP)
             for w in range(2):
@@ -178,31 +174,42 @@ def tile_list_concrete_recipe_scores_kernel(
                         nc.tensor.matmul_mx(
                             out=acc[:, x * STEP:(x + 1) * STEP],
                             lhsT=w4_w[b][:, a, i, :].bitcast(FP4X4), lhsT_scale=w4_s[b][:, a, i, :],
-                            rhs=v_words(a, cols.start, cols.stop).bitcast(FP8X4), rhs_scale=v_s[a][:, cols],
+                            rhs=v_words(a, cols.start, cols.stop).bitcast(FP8X4), rhs_scale=(v_s, v_s_low)[a][:, cols],
                             start=(a == 0 and x == 0), stop=(a == PASSES - 1 and x == 1))
                 b_banks.append(acc)
             square = reused("square", "square%d" % n, [P, PACK, STEP], F32)
             size = reused("size", "size%d" % (n % 4), [P, PACK, STEP], F32)
+            def root(lo, hi):
+                for i in range(PACK):
+                    nc.scalar.activation(
+                        out=size[:, i, lo:hi], in_=square[:, i, lo:hi], func=ACT.Sqrt, bias=unit_t[:, b, i:i + 1])
+
             for u in range(2):
                 nc.scalar.activation(
                     out=square[:, :, u * HALF:(u + 1) * HALF],
                     in_=st_banks[u][:].rearrange("p (i j) -> p i j", i=PACK), func=ACT.Square)
-            for i in range(PACK):
-                nc.scalar.activation(
-                    out=size[:, i, :], in_=square[:, i, :], func=ACT.Sqrt, bias=unit_t[:, b, i:i + 1])
+                if n == 0:
+                    root(u * HALF, (u + 1) * HALF)
+            if n > 0:
+                root(0, STEP)
             scaled = ring.tile([P, PACK, STEP], F32, name="scaled")
-            h_bf = ring.tile([P, STEP * PACK], BF16, name="h_bf", align_bytes=64)
+            if n == PASSES * STEPS - 1:
+                h_bf = [reused("h_bf_last", "h_bf_last%d" % (1 - u), [P, HALF * PACK], BF16)[:] for u in range(2)]
+            else:
+                whole = ring.tile([P, STEP * PACK], BF16, name="h_bf", align_bytes=64)
+                h_bf = [whole[:, 0:HALF * PACK], whole[:, HALF * PACK:STEP * PACK], whole[:]]
             state[n] = (st_banks, b_banks, size, scaled, h_bf)
 
-        def scale_step(n, w):
+        def scale_step(n, w, lo=0, hi=STEP):
             st_banks, b_banks, size, scaled, h_bf = state[n]
             nc.vector.tensor_tensor(
-                scaled[:, 2 * w:2 * w + 2, :].rearrange("p x j -> p (x j)"), b_banks[w][:],
-                size[:, 2 * w:2 * w + 2, :].rearrange("p x j -> p (x j)"), ALU.mult)
+                scaled[:, 2 * w:2 * w + 2, lo:hi],
+                b_banks[w][:].rearrange("p (x j) -> p x j", x=2)[:, :, lo:hi],
+                size[:, 2 * w:2 * w + 2, lo:hi], ALU.mult)
 
         def skip_step(n, u):
             st_banks, b_banks, size, scaled, h_bf = state[n]
-            dst = h_bf[:, u * HALF * PACK:(u + 1) * HALF * PACK]
+            dst = h_bf[u]
             nc.vector.tensor_tensor(
                 dst.rearrange("p (g j i) -> p g i j", j=4, i=PACK),
                 st_banks[u][:].rearrange("p (i g j) -> p g i j", i=PACK, j=4),
@@ -215,7 +222,7 @@ def tile_list_concrete_recipe_scores_kernel(
             cols = slice(c * STEP + lo, c * STEP + hi)
             nc.vector.quantize_mx(
                 out=h_w[b][:, cols].bitcast(FP8X4), scales=h_s[b][:, cols],
-                in_=h_bf[:, lo * PACK:hi * PACK])
+                in_=h_bf[2] if hi - lo == STEP else h_bf[lo // HALF])
 
         def score(m, lo, hi, tag, depth):
             acc = bank(tag, depth)
@@ -223,55 +230,83 @@ def tile_list_concrete_recipe_scores_kernel(
             for b in range(PASSES):
                 nc.tensor.matmul_mx(
                     out=acc[:, 0:hi - lo],
-                    lhsT=late["v2_w", b][:, rows].bitcast(FP8X4), lhsT_scale=late["v2_s"][4 * b:P, rows],
+                    lhsT=late["v2_w", b, m // 2][:, (m % 2) * P:(m % 2 + 1) * P].bitcast(FP8X4), lhsT_scale=late["v2_s"][4 * b:P, rows],
                     rhs=h_w[b][:, lo:hi].bitcast(FP8X4), rhs_scale=h_s[b][:, lo:hi],
                     start=(b == 0), stop=(b == PASSES - 1))
             nc.scalar.copy(out=scores[m][:, lo:hi], in_=acc[:, 0:hi - lo])
 
+        warm = held("warm", [P, 2], F32)
+        nc.vector.memset(warm[:, 0:1], 1.0)
+        nc.scalar.activation(out=warm[:, 1:2], in_=warm[:, 0:1], func=ACT.Sqrt)
         round_w1("scalar", 0, 0, 0, P)
-        for a in range(PASSES):
-            gather(v_s[a][:], tab_s[:, a * T:(a + 1) * T], offs_t, 0, S)
+        gather(v_s[:], tab_s[:], offs_t, 0, S)
+        for q in range(4):
+            nc.sync.dma_start(
+                out=v_s_low[32 * q:32 * q + 4, :].bitcast(I32), in_=v_s[32 * q + 4:32 * q + 8, :].bitcast(I32))
+        load_w4(1)
+        load_w1(1, 0)
+        load_w1(1, 1)
+        for q in range(4):
+            nc.sync.dma_start(
+                out=tab2_s[32 * q:32 * q + 8, :].bitcast(I32),
+                in_=tab2_scales[:, 4 * q:4 * q + 4, :].bitcast(I32))
+        load_words(tab2_w[0], tab2_words[0])
+        load_words(tab2_w[1], tab2_words[1])
+        nc.sync.dma_start(pos1_t[:], pos1)
+        nc.sync.dma_start(pos2_t[:], pos2)
+        nc.sync.dma_start(out=req_t[:], in_=req.rearrange("(m p) j -> p m j", p=P))
         gather(v_w0[:], tab_w[0][:], offs_t, 0, S)
         quantize_w1(0, 0)
-        round_w1("scalar", 0, 1, 0, P)
-        gather(v_w1_first[:], tab_w[1][:], offs_t, 0, STEP)
+        round_w1("scalar", 0, 1, 0, 64)
+        round_w1("vector", 0, 1, 64, P)
         quantize_w1(0, 1)
+        gather(v_w1_first[:], tab_w[1][:], offs_t, 0, STEP)
         late["v_w1"] = reused("v_w1", "w1_bf01", [P, S - STEP], U32)
         for c in range(1, STEPS):
             gather(v_words(1, c * STEP, (c + 1) * STEP), tab_w[1][:], offs_t, c * STEP, (c + 1) * STEP)
+        w4_w[0] = shared.tile([P, PASSES, PACK, 2 * P], U8, name="w4_w0", align_bytes=64, offset=0)
         deal_w4(0)
         for lo in range(0, P, 32):
             round_w1("gpsimd", 1, 0, lo, lo + 32)
 
         last = PASSES * STEPS - 1
-        for n in range(last + 1):
+        products(0)
+        for u in range(2):
+            for w in range(2):
+                scale_step(0, w, u * HALF, (u + 1) * HALF)
+        skip_step(0, 0)
+        w1_bf[1, 1] = reused("w1_bf11", "square0", [P, PACK * KP], BF16)
+        round_w1("scalar", 1, 1, 0, 32)
+        round_w1("gpsimd", 1, 1, 96, P)
+        for n in range(1, last + 1):
             products(n)
             scale_step(n, 0)
-            if n > 0:
-                skip_step(n - 1, 1)
+            if n == 2:
+                quantize_w1(1, 1)
+            skip_step(n - 1, 1)
             scale_step(n, 1)
-            if n > 0:
-                quantize_h(n - 1, 0, STEP)
+            quantize_h(n - 1, 0, STEP)
             skip_step(n, 0)
-            if n == 0:
-                w1_bf[1, 1] = reused("w1_bf11", "square0", [P, PACK * KP], BF16)
-                round_w1("scalar", 1, 1, 0, 32)
-                deal_w4(1)
             if n == 1:
                 round_w1("scalar", 1, 1, 32, 64)
-                round_w1("vector", 1, 1, 64, P)
+                round_w1("vector", 1, 1, 64, 96)
                 w1_w[1, 0] = reused("w1_w10", "square1", [P, KP], U32)
                 quantize_w1(1, 0)
-                quantize_w1(1, 1)
+            if n == 2:
+                w4_w[1] = reused("w4_w1", "square2", [P, PASSES, PACK, 2 * P], U8)
+                deal_w4(1)
             if n == 4:
                 late["v2_s"] = reused("v2_s", "square3", [P, S2], U8)
                 gather(late["v2_s"][:], tab2_s[:], offs2_t, 0, S2)
             if n in (5, 6):
-                late["v2_w", n - 5] = reused("v2_w", "square%d" % (n - 1), [P, S2], U32)
-                gather(late["v2_w", n - 5][:], tab2_w[n - 5][:], offs2_t, 0, S2)
-        skip_step(last, 1)
+                late["v2_w", n - 5, 0] = reused("v2_w", "square%d" % (n - 1), [P, S2 // 2], U32)
+                gather(late["v2_w", n - 5, 0][:], tab2_w[n - 5][:], offs2_t, 0, S2 // 2)
         quantize_h(last, 0, HALF)
+        skip_step(last, 1)
         quantize_h(last, HALF, STEP)
+        for b in range(PASSES):
+            late["v2_w", b, 1] = reused("v2_w_tail", "h_bf_last%d" % b, [P, S2 // 2], U32)
+            gather(late["v2_w", b, 1][:], tab2_w[b][:], offs2_t, S2 // 2, S2)
 
         for lo, hi in ((0, 512), (512, 768), (768, 896), (896, 1024)):
             score(0, lo, hi, "bb", 3)

@@ -62,11 +62,11 @@ def tile_list_concrete_recipe_scores_kernel(
         w4_raw = per("w4_raw", PASSES, [P, PASSES, 2 * KP], U8)
         w4_raw_s = held("w4_raw_s", [P, PASSES, H], U8)
         w4_w = {}
-        w4_s = per("w4_s", PASSES, [P, PASSES, PACK, P], U8)
+        w4_s = {0: held("w4_s0", [P, PASSES, PACK, P], U8)}
         w1_raw = {(b, a): held("w1_raw%d%d" % (b, a), [P, PACK, KP], F32) for b, a in ((0, 0), (1, 0), (1, 1))}
         w1_raw[0, 1] = shared.tile([P, PACK, KP], F32, name="w1_raw01", align_bytes=64, offset=0)
-        w1_bf = {(b, a): held("w1_bf%d%d" % (b, a), [P, PACK * KP], BF16) for b, a in ((0, 0), (0, 1), (1, 0))}
-        w1_w = {(b, a): held("w1_w%d%d" % (b, a), [P, KP], U32) for b, a in ((0, 0), (0, 1), (1, 1))}
+        w1_bf = {(b, a): held("w1_bf%d%d" % (b, a), [P, PACK * KP], BF16) for b, a in ((0, 0), (0, 1))}
+        w1_w = {(b, a): held("w1_w%d%d" % (b, a), [P, KP], U32) for b in range(PASSES) for a in range(PASSES)}
         late = {}
         w1_s = [per("w1_s%d_" % b, PASSES, [P, KP], U8) for b in range(PASSES)]
         unit_t = held("unit_t", [P, PASSES, PACK], F32)
@@ -99,13 +99,13 @@ def tile_list_concrete_recipe_scores_kernel(
                 out=tab_s[32 * q:32 * q + 8, :].bitcast(I32),
                 in_=tab_scales[:, 4 * q:4 * q + 4, :].bitcast(I32))
         load_w1(0, 0)
-        load_w1(0, 1)
-        load_words(tab_w[1], tab_words[1])
-        load_w4(0)
         for q in range(4):
             nc.sync.dma_start(
                 out=w4_raw_s[32 * q:32 * q + 4, :, :].bitcast(I32),
                 in_=w4_scales[:, 4 * q:4 * q + 4, :].rearrange("a r c -> r a c").bitcast(I32))
+        load_w1(0, 1)
+        load_words(tab_w[1], tab_words[1])
+        load_w4(0)
         nc.sync.dma_start(out=unit_t[:], in_=unit2.rearrange("(b p i) -> p b i", b=PASSES, i=PACK))
 
         def v_words(a, lo, hi):
@@ -123,7 +123,9 @@ def tile_list_concrete_recipe_scores_kernel(
             nc.scalar.copy(
                 out=w4_w[b][:].bitcast(U16),
                 in_=w4_raw[b][:].bitcast(U16).rearrange("p a (m i) -> p a i m", i=PACK))
-            nc.gpsimd.tensor_copy(
+
+        def deal_w4_scales(engine, b):
+            engine.tensor_copy(
                 out=w4_s[b][:],
                 in_=w4_raw_s[:, :, b * KP:(b + 1) * KP].rearrange("p a (m i) -> p a i m", i=PACK))
 
@@ -132,11 +134,8 @@ def tile_list_concrete_recipe_scores_kernel(
             src = w1_raw[b, a][:].rearrange("p j (m i) -> p m j i", i=PACK)[:, lo:hi]
             if engine == "scalar":
                 nc.scalar.copy(out=dst, in_=src)
-            elif engine == "vector":
-                nc.vector.tensor_copy(out=dst, in_=src)
             else:
-                nc.gpsimd.tensor_copy(
-                    out=dst.rearrange("p m j i -> p i m j"), in_=src.rearrange("p m j i -> p i m j"))
+                nc.vector.tensor_copy(out=dst, in_=src)
 
         def quantize_w1(b, a):
             nc.vector.quantize_mx(out=w1_w[b, a][:].bitcast(FP8X4), scales=w1_s[b][a][:], in_=w1_bf[b, a][:])
@@ -243,9 +242,9 @@ def tile_list_concrete_recipe_scores_kernel(
         for q in range(4):
             nc.sync.dma_start(
                 out=v_s_low[32 * q:32 * q + 4, :].bitcast(I32), in_=v_s[32 * q + 4:32 * q + 8, :].bitcast(I32))
-        load_w4(1)
         load_w1(1, 0)
         load_w1(1, 1)
+        load_w4(1)
         for q in range(4):
             nc.sync.dma_start(
                 out=tab2_s[32 * q:32 * q + 8, :].bitcast(I32),
@@ -256,6 +255,7 @@ def tile_list_concrete_recipe_scores_kernel(
         nc.sync.dma_start(pos2_t[:], pos2)
         nc.sync.dma_start(out=req_t[:], in_=req.rearrange("(m p) j -> p m j", p=P))
         gather(v_w0[:], tab_w[0][:], offs_t, 0, S)
+        deal_w4_scales(nc.vector, 0)
         quantize_w1(0, 0)
         round_w1("scalar", 0, 1, 0, 64)
         round_w1("vector", 0, 1, 64, P)
@@ -266,8 +266,6 @@ def tile_list_concrete_recipe_scores_kernel(
             gather(v_words(1, c * STEP, (c + 1) * STEP), tab_w[1][:], offs_t, c * STEP, (c + 1) * STEP)
         w4_w[0] = shared.tile([P, PASSES, PACK, 2 * P], U8, name="w4_w0", align_bytes=64, offset=0)
         deal_w4(0)
-        for lo in range(0, P, 32):
-            round_w1("gpsimd", 1, 0, lo, lo + 32)
 
         last = PASSES * STEPS - 1
         products(0)
@@ -275,23 +273,24 @@ def tile_list_concrete_recipe_scores_kernel(
             for w in range(2):
                 scale_step(0, w, u * HALF, (u + 1) * HALF)
         skip_step(0, 0)
-        w1_bf[1, 1] = reused("w1_bf11", "square0", [P, PACK * KP], BF16)
-        round_w1("scalar", 1, 1, 0, 32)
-        round_w1("gpsimd", 1, 1, 96, P)
+        w1_bf[1, 0] = reused("w1_bf10", "square0", [P, PACK * KP], BF16)
+        round_w1("scalar", 1, 0, 0, 64)
+        round_w1("vector", 1, 0, 64, P)
         for n in range(1, last + 1):
             products(n)
             scale_step(n, 0)
-            if n == 2:
-                quantize_w1(1, 1)
             skip_step(n - 1, 1)
             scale_step(n, 1)
+            if n in (1, 2):
+                quantize_w1(1, n - 1)
             quantize_h(n - 1, 0, STEP)
             skip_step(n, 0)
             if n == 1:
-                round_w1("scalar", 1, 1, 32, 64)
-                round_w1("vector", 1, 1, 64, 96)
-                w1_w[1, 0] = reused("w1_w10", "square1", [P, KP], U32)
-                quantize_w1(1, 0)
+                w1_bf[1, 1] = reused("w1_bf11", "square1", [P, PACK * KP], BF16)
+                round_w1("scalar", 1, 1, 0, 96)
+                round_w1("vector", 1, 1, 96, P)
+                w4_s[1] = reused("w4_s1", "w1_raw10", [P, PASSES, PACK, P], U8)
+                deal_w4_scales(nc.gpsimd, 1)
             if n == 2:
                 w4_w[1] = reused("w4_w1", "square2", [P, PASSES, PACK, 2 * P], U8)
                 deal_w4(1)

from contextlib import ExitStack

import concourse.mybir as mybir

K, T, H, S, T3, S2, PAIRS = 1024, 2048, 1024, 1024, 2048, 512, 512
FLOPS = 2 * (2 * K * H * S + H * S2 * S)

F32 = mybir.dt.float32
BF16 = mybir.dt.bfloat16
I32 = mybir.dt.int32
U32 = mybir.dt.uint32
U16 = mybir.dt.uint16
U8 = mybir.dt.uint8
FP8X4 = mybir.dt.float8_e4m3fn_x4
FP4X4 = mybir.dt.float4_e2m1fn_x4
ACT = mybir.ActivationFunctionType
ALU = mybir.AluOpType

P = 128
PACK = 4
KP = P * PACK
PASSES = 2
STEP = 256
STEPS = S // STEP
HALF = STEP // 2
LIST_COL = 16


def tile_list_concrete_recipe_scores_kernel(
    tc, tab_words, tab_scales, offs, w1, w4_words, w4_scales, unit2,
    tab2_words, tab2_scales, offs2, pos1, pos2, req, out,
):
    nc = tc.nc
    with ExitStack() as ctx:
        keep = ctx.enter_context(tc.tile_pool(name="keep", bufs=1))
        ring = ctx.enter_context(tc.tile_pool(name="ring", bufs=3))
        shared = ctx.enter_context(tc.tile_pool(name="shared", bufs=1))
        psum = ctx.enter_context(tc.psum_pool(name="psum", bufs=1))

        def held(name, shape, dtype):
            return keep.tile(shape, dtype, name=name, align_bytes=64)

        def reused(name, tag, shape, dtype):
            return keep.tile(shape, dtype, name=name, tag=tag, align_bytes=64)

        def per(name, count, shape, dtype):
            return [held("%s%d" % (name, n), shape, dtype) for n in range(count)]

        offs_t = held("offs_t", [P, S // LIST_COL], U16)
        offs2_t = held("offs2_t", [P, S2 // LIST_COL], U16)
        pos1_t = held("pos1_t", [P, PAIRS // LIST_COL], U16)
        pos2_t = held("pos2_t", [P, PAIRS // LIST_COL], U16)

        tab_w = per("tab_w", PASSES, [P, T], U32)
        tab_s = held("tab_s", [P, T], U8)
        tab2_w = per("tab2_w", PASSES, [P, T3], U32)
        tab2_s = held("tab2_s", [P, T3], U8)
        v_w0 = held("v_w0", [P, S], U32)
        v_w1_first = held("v_w1_first", [P, STEP], U32)
        v_s = held("v_s", [P, S], U8)
        v_s_low = held("v_s_low", [P, S], U8)
        w4_raw = per("w4_raw", PASSES, [P, PASSES, 2 * KP], U8)
        w4_raw_s = held("w4_raw_s", [P, PASSES, H], U8)
        w4_w = {}
        w4_s = {0: held("w4_s0", [P, PASSES, PACK, P], U8)}
        w1_raw = {(b, a): held("w1_raw%d%d" % (b, a), [P, PACK, KP], F32) for b, a in ((0, 0), (1, 0), (1, 1))}
        w1_raw[0, 1] = shared.tile([P, PACK, KP], F32, name="w1_raw01", align_bytes=64, offset=0)
        w1_bf = {(b, a): held("w1_bf%d%d" % (b, a), [P, PACK * KP], BF16) for b, a in ((0, 0), (0, 1))}
        w1_w = {(b, a): held("w1_w%d%d" % (b, a), [P, KP], U32) for b in range(PASSES) for a in range(PASSES)}
        late = {}
        w1_s = [per("w1_s%d_" % b, PASSES, [P, KP], U8) for b in range(PASSES)]
        unit_t = held("unit_t", [P, PASSES, PACK], F32)
        h_w = per("h_w", PASSES, [P, S], U32)
        h_s = per("h_s", PASSES, [P, S], U8)
        scores = per("scores", S2 // P, [P, S], F32)
        req_t = held("req_t", [P, S2 // P, PAIRS], F32)

        def load_words(dst, src):
            nc.sync.dma_start(out=dst[:].bitcast(I32), in_=src.rearrange("p t i -> p (t i)").bitcast(I32))

        def load_w1(b, a):
            rows = w1[a * KP:(a + 1) * KP, b * KP:(b + 1) * KP]
            nc.sync.dma_start(out=w1_raw[b, a][:], in_=rows.rearrange("(p j) c -> p j c", j=PACK))

        def load_w4(b):
            src = w4_words[:, :, 2 * KP * b:2 * KP * (b + 1)].rearrange("a p c -> p a c")
            nc.sync.dma_start(out=w4_raw[b][:].bitcast(I32), in_=src.bitcast(I32))

        nc.gpsimd.memset(tab_s[:].bitcast(I32), 0)
        nc.gpsimd.memset(w4_raw_s[:].rearrange("p a c -> p (a c)").bitcast(I32), 0)
        nc.gpsimd.memset(v_s_low[:].bitcast(I32), 0)
        nc.gpsimd.memset(tab2_s[:].bitcast(I32), 0)

        nc.sync.dma_start(offs_t[:], offs)
        load_words(tab_w[0], tab_words[0])
        nc.sync.dma_start(offs2_t[:], offs2)
        for q in range(4):
            nc.sync.dma_start(
                out=tab_s[32 * q:32 * q + 8, :].bitcast(I32),
                in_=tab_scales[:, 4 * q:4 * q + 4, :].bitcast(I32))
        load_w1(0, 0)
        for q in range(4):
            nc.sync.dma_start(
                out=w4_raw_s[32 * q:32 * q + 4, :, :].bitcast(I32),
                in_=w4_scales[:, 4 * q:4 * q + 4, :].rearrange("a r c -> r a c").bitcast(I32))
        load_w1(0, 1)
        load_words(tab_w[1], tab_words[1])
        load_w4(0)
        nc.sync.dma_start(out=unit_t[:], in_=unit2.rearrange("(b p i) -> p b i", b=PASSES, i=PACK))

        def v_words(a, lo, hi):
            if a == 0:
                return v_w0[:, lo:hi]
            if hi <= STEP:
                return v_w1_first[:, lo:hi]
            return late["v_w1"][:, lo - STEP:hi - STEP]

        def gather(dst, window, offsets, lo, hi):
            nc.vector.tensor_copy(
                dst, window.indirect(offsets[:, lo // LIST_COL:hi // LIST_COL]))

        def deal_w4(b):
            nc.scalar.copy(
                out=w4_w[b][:].bitcast(U16),
                in_=w4_raw[b][:].bitcast(U16).rearrange("p a (m i) -> p a i m", i=PACK))

        def deal_w4_scales(engine, b):
            engine.tensor_copy(
                out=w4_s[b][:],
                in_=w4_raw_s[:, :, b * KP:(b + 1) * KP].rearrange("p a (m i) -> p a i m", i=PACK))

        def round_w1(engine, b, a, lo, hi):
            dst = w1_bf[b, a][:].rearrange("p (i m j) -> p m j i", i=PACK, j=PACK)[:, lo:hi]
            src = w1_raw[b, a][:].rearrange("p j (m i) -> p m j i", i=PACK)[:, lo:hi]
            if engine == "scalar":
                nc.scalar.copy(out=dst, in_=src)
            else:
                nc.vector.tensor_copy(out=dst, in_=src)

        def quantize_w1(b, a):
            nc.vector.quantize_mx(out=w1_w[b, a][:].bitcast(FP8X4), scales=w1_s[b][a][:], in_=w1_bf[b, a][:])

        def bank(tag, depth):
            return psum.tile([P, 512], F32, name=tag, tag=tag, bufs=depth)

        state = {}

        def products(n):
            b, c = divmod(n, STEPS)
            st_banks, b_banks = [], []
            for u in range(2):
                acc = bank("st", 5)
                cols = slice(c * STEP + u * HALF, c * STEP + (u + 1) * HALF)
                if n == 0:
                    order = [(a, i) for a in range(PASSES) for i in range(PACK)]
                else:
                    order = [(a, i) for i in range(PACK) for a in range(PASSES)]
                for a, i in order:
                    nc.tensor.matmul_mx(
                        out=acc[:, i * HALF:(i + 1) * HALF],
                        lhsT=w1_w[b, a][:, i * P:(i + 1) * P].bitcast(FP8X4),
                        lhsT_scale=w1_s[b][a][:, i * P:(i + 1) * P],
                        rhs=v_words(a, cols.start, cols.stop).bitcast(FP8X4),
                        rhs_scale=v_s[4 * a:P, cols],
                        start=((a, i) == order[0]), stop=((a, i) == order[-1]))
                st_banks.append(acc)
            cols = slice(c * STEP, (c + 1) * STEP)
            for w in range(2):
                acc = bank("bb", 3)
                for a in range(PASSES):
                    for x in range(2):
                        i = 2 * w + x
                        nc.tensor.matmul_mx(
                            out=acc[:, x * STEP:(x + 1) * STEP],
                            lhsT=w4_w[b][:, a, i, :].bitcast(FP4X4), lhsT_scale=w4_s[b][:, a, i, :],
                            rhs=v_words(a, cols.start, cols.stop).bitcast(FP8X4), rhs_scale=(v_s, v_s_low)[a][:, cols],
                            start=(a == 0 and x == 0), stop=(a == PASSES - 1 and x == 1))
                b_banks.append(acc)
            square = reused("square", "square%d" % n, [P, PACK, STEP], F32)
            size = reused("size", "size%d" % (n % 4), [P, PACK, STEP], F32)
            def root(lo, hi):
                for i in range(PACK):
                    nc.scalar.activation(
                        out=size[:, i, lo:hi], in_=square[:, i, lo:hi], func=ACT.Sqrt, bias=unit_t[:, b, i:i + 1])

            for u in range(2):
                nc.scalar.activation(
                    out=square[:, :, u * HALF:(u + 1) * HALF],
                    in_=st_banks[u][:].rearrange("p (i j) -> p i j", i=PACK), func=ACT.Square)
                if n == 0:
                    root(u * HALF, (u + 1) * HALF)
            if n > 0:
                root(0, STEP)
            scaled = ring.tile([P, PACK, STEP], F32, name="scaled")
            if n == PASSES * STEPS - 1:
                h_bf = [reused("h_bf_last", "h_bf_last%d" % (1 - u), [P, HALF * PACK], BF16)[:] for u in range(2)]
            else:
                whole = ring.tile([P, STEP * PACK], BF16, name="h_bf", align_bytes=64)
                h_bf = [whole[:, 0:HALF * PACK], whole[:, HALF * PACK:STEP * PACK], whole[:]]
            state[n] = (st_banks, b_banks, size, scaled, h_bf)

        def scale_step(n, w, lo=0, hi=STEP):
            st_banks, b_banks, size, scaled, h_bf = state[n]
            nc.vector.tensor_tensor(
                scaled[:, 2 * w:2 * w + 2, lo:hi],
                b_banks[w][:].rearrange("p (x j) -> p x j", x=2)[:, :, lo:hi],
                size[:, 2 * w:2 * w + 2, lo:hi], ALU.mult)

        def skip_step(n, u):
            st_banks, b_banks, size, scaled, h_bf = state[n]
            dst = h_bf[u]
            nc.vector.tensor_tensor(
                dst.rearrange("p (g j i) -> p g i j", j=4, i=PACK),
                st_banks[u][:].rearrange("p (i g j) -> p g i j", i=PACK, j=4),
                scaled[:, :, u * HALF:(u + 1) * HALF].rearrange("p i (g j) -> p g i j", j=4),
                ALU.add)

        def quantize_h(n, lo, hi):
            b, c = divmod(n, STEPS)
            h_bf = state[n][4]
            cols = slice(c * STEP + lo, c * STEP + hi)
            nc.vector.quantize_mx(
                out=h_w[b][:, cols].bitcast(FP8X4), scales=h_s[b][:, cols],
                in_=h_bf[2] if hi - lo == STEP else h_bf[lo // HALF])

        def score(m, lo, hi, tag, depth):
            acc = bank(tag, depth)
            rows = slice(m * P, (m + 1) * P)
            for b in range(PASSES):
                nc.tensor.matmul_mx(
                    out=acc[:, 0:hi - lo],
                    lhsT=late["v2_w", b, m // 2][:, (m % 2) * P:(m % 2 + 1) * P].bitcast(FP8X4), lhsT_scale=late["v2_s"][4 * b:P, rows],
                    rhs=h_w[b][:, lo:hi].bitcast(FP8X4), rhs_scale=h_s[b][:, lo:hi],
                    start=(b == 0), stop=(b == PASSES - 1))
            nc.scalar.copy(out=scores[m][:, lo:hi], in_=acc[:, 0:hi - lo])

        warm = held("warm", [P, 2], F32)
        nc.vector.memset(warm[:, 0:1], 1.0)
        nc.scalar.activation(out=warm[:, 1:2], in_=warm[:, 0:1], func=ACT.Sqrt)
        round_w1("scalar", 0, 0, 0, P)
        gather(v_s[:], tab_s[:], offs_t, 0, S)
        for q in range(4):
            nc.sync.dma_start(
                out=v_s_low[32 * q:32 * q + 4, :].bitcast(I32), in_=v_s[32 * q + 4:32 * q + 8, :].bitcast(I32))
        load_w1(1, 0)
        load_w1(1, 1)
        load_w4(1)
        for q in range(4):
            nc.sync.dma_start(
                out=tab2_s[32 * q:32 * q + 8, :].bitcast(I32),
                in_=tab2_scales[:, 4 * q:4 * q + 4, :].bitcast(I32))
        load_words(tab2_w[0], tab2_words[0])
        load_words(tab2_w[1], tab2_words[1])
        nc.sync.dma_start(pos1_t[:], pos1)
        nc.sync.dma_start(pos2_t[:], pos2)
        nc.sync.dma_start(out=req_t[:], in_=req.rearrange("(m p) j -> p m j", p=P))
        gather(v_w0[:], tab_w[0][:], offs_t, 0, S)
        deal_w4_scales(nc.vector, 0)
        quantize_w1(0, 0)
        round_w1("scalar", 0, 1, 0, 64)
        round_w1("vector", 0, 1, 64, P)
        quantize_w1(0, 1)
        gather(v_w1_first[:], tab_w[1][:], offs_t, 0, STEP)
        late["v_w1"] = reused("v_w1", "w1_bf01", [P, S - STEP], U32)
        for c in range(1, STEPS):
            gather(v_words(1, c * STEP, (c + 1) * STEP), tab_w[1][:], offs_t, c * STEP, (c + 1) * STEP)
        w4_w[0] = shared.tile([P, PASSES, PACK, 2 * P], U8, name="w4_w0", align_bytes=64, offset=0)
        deal_w4(0)

        last = PASSES * STEPS - 1
        products(0)
        for u in range(2):
            for w in range(2):
                scale_step(0, w, u * HALF, (u + 1) * HALF)
        skip_step(0, 0)
        w1_bf[1, 0] = reused("w1_bf10", "square0", [P, PACK * KP], BF16)
        round_w1("scalar", 1, 0, 0, 64)
        round_w1("vector", 1, 0, 64, P)
        for n in range(1, last + 1):
            products(n)
            scale_step(n, 0)
            skip_step(n - 1, 1)
            scale_step(n, 1)
            if n in (1, 2):
                quantize_w1(1, n - 1)
            quantize_h(n - 1, 0, STEP)
            skip_step(n, 0)
            if n == 1:
                w1_bf[1, 1] = reused("w1_bf11", "square1", [P, PACK * KP], BF16)
                round_w1("scalar", 1, 1, 0, 96)
                round_w1("vector", 1, 1, 96, P)
                w4_s[1] = reused("w4_s1", "w1_raw10", [P, PASSES, PACK, P], U8)
                deal_w4_scales(nc.gpsimd, 1)
            if n == 2:
                w4_w[1] = reused("w4_w1", "square2", [P, PASSES, PACK, 2 * P], U8)
                deal_w4(1)
            if n == 4:
                late["v2_s"] = reused("v2_s", "square3", [P, S2], U8)
                gather(late["v2_s"][:], tab2_s[:], offs2_t, 0, S2)
            if n in (5, 6):
                late["v2_w", n - 5, 0] = reused("v2_w", "square%d" % (n - 1), [P, S2 // 2], U32)
                gather(late["v2_w", n - 5, 0][:], tab2_w[n - 5][:], offs2_t, 0, S2 // 2)
        quantize_h(last, 0, HALF)
        skip_step(last, 1)
        quantize_h(last, HALF, STEP)
        for b in range(PASSES):
            late["v2_w", b, 1] = reused("v2_w_tail", "h_bf_last%d" % b, [P, S2 // 2], U32)
            gather(late["v2_w", b, 1][:], tab2_w[b][:], offs2_t, S2 // 2, S2)

        for lo, hi in ((0, 512), (512, 768), (768, 896), (896, 1024)):
            score(0, lo, hi, "bb", 3)
        for m in range(1, S2 // P):
            for lo in (0, 512):
                score(m, lo, lo + 512, "st", 5)

        for m in range(S2 // P):
            pieces = 2 if m == S2 // P - 1 else 1
            width = PAIRS // pieces
            for lo in range(0, PAIRS, width):
                cols = slice(lo, lo + width)
                part = slice(lo // LIST_COL, (lo + width) // LIST_COL)
                early = ring.tile([P, width], F32, name="early")
                later = ring.tile([P, width], F32, name="later")
                best = ring.tile([P, width], F32, name="best")
                nc.vector.tensor_tensor(early[:], scores[m][:].indirect(pos1_t[:, part]), req_t[:, m, cols], ALU.add)
                nc.vector.tensor_tensor(later[:], scores[m][:].indirect(pos2_t[:, part]), req_t[:, m, cols], ALU.add)
                nc.vector.tensor_tensor(best[:], early[:], later[:], ALU.max)
                nc.sync.dma_start(out=out[m * P:(m + 1) * P, cols], in_=best[:])
